import numpy as np
import ml_dtypes


def mxq(x, axis, fmt="e4m3"):
    dtype, down = {"e4m3": (ml_dtypes.float8_e4m3fn, 7), "e5m2": (ml_dtypes.float8_e5m2, 14)}[fmt]
    v = np.moveaxis(np.asarray(x, np.float32).astype(ml_dtypes.bfloat16).astype(np.float64), axis, -1)
    blocks = v.reshape(v.shape[:-1] + (-1, 32))
    amax = np.abs(blocks).max(-1, keepdims=True)
    byte = np.maximum(np.where(amax > 0, np.frexp(amax)[1] - 1 + 127, 0) - down, 1)
    scale = np.exp2(byte - 127.0)
    codes = (blocks / scale).astype(np.float32).astype(dtype).astype(np.float64)
    return np.moveaxis((codes * scale).reshape(v.shape), -1, axis)


WIDE = False


def mx_kscale(k):
    if not WIDE:
        return np.ones(k)
    levels = np.array([10, -10, 5, -5, 0])
    if k % 512:
        return np.exp2(np.random.permutation(np.resize(levels, k // 32))).repeat(32)
    a = np.empty((k // 512, 16))
    for p in range(k // 512):
        a[p, :8] = np.random.permutation(np.resize(levels, 8))
        for g in range(8):
            far = levels[np.abs(levels - a[p, g]) >= 10]
            a[p, g + 8] = far[np.random.randint(len(far))]
    return np.exp2(a.ravel()).repeat(32)


def f64(x):
    return np.asarray(x).astype(np.float64)


def striped8(idx):
    return np.asarray(idx).reshape(8, -1, 16).transpose(0, 2, 1).reshape(128, -1).astype(np.uint16)


def unstriped8(offs):
    return offs.reshape(8, 16, -1).transpose(0, 2, 1).reshape(8, -1).astype(np.int64)


def pick8(x, idx, run):
    r = np.arange(len(x))
    return x[r[:, None], idx[r % (8 * run) // run]]


E2M1 = np.array([0.0, 0.5, 1.0, 1.5, 2.0, 3.0, 4.0, 6.0, -0.0, -0.5, -1.0, -1.5, -2.0, -3.0, -4.0, -6.0])


def pack_weight(w, fmt):
    k, n = w.shape
    w = f64(np.asarray(w, np.float32).astype(ml_dtypes.bfloat16)).reshape(k // 32, 32, n)
    amax = np.abs(w).max(1)
    if fmt == "e4m3":
        byte = np.frexp(amax)[1] - 1 + 127 - 7
    else:
        mant, ex = np.frexp(amax / 6.0)
        byte = np.where(mant > 0.5, ex, ex - 1) + 127
    byte = np.clip(np.where(amax > 0, byte, 1), 1, 254)
    scaled = (w * np.exp2(127.0 - byte)[:, None, :]).reshape(k, n).astype(np.float32)
    by_word = np.ascontiguousarray(scaled.reshape(k // 512, 128, 4, n).transpose(0, 1, 3, 2))
    if fmt == "e4m3":
        words = by_word.astype(ml_dtypes.float8_e4m3fn).view(np.uint8)
    else:
        c = by_word.astype(ml_dtypes.float4_e2m1fn).view(np.uint8) & 0xF
        words = (c[..., 0::2] | (c[..., 1::2] << 4)).reshape(k // 512, 128, 2 * n)
    return np.ascontiguousarray(words), np.ascontiguousarray(byte.astype(np.uint8).reshape(k // 512, 16, n))


def unpack_weight(words, scales, fmt):
    g, _, n = scales.shape
    words = np.ascontiguousarray(words).reshape(g, 128, n, -1)
    if fmt == "e4m3":
        vals = words.view(ml_dtypes.float8_e4m3fn).astype(np.float64)
    else:
        nib = np.empty((g, 128, n, 4), np.uint8)
        nib[..., 0::2] = words & 0xF
        nib[..., 1::2] = words >> 4
        vals = E2M1[nib]
    vals = vals * np.repeat(np.exp2(scales.astype(np.float64) - 127.0), 8, axis=1)[..., None]
    return vals.transpose(0, 1, 3, 2).reshape(g * 512, n)


def softplus(v):
    return np.log(1.0 + np.exp(v))


D, T, I, Q = 512, 1024, 512, 128


def setup_inputs():
    n = np.random.standard_normal
    idx = np.stack([np.random.permutation(T)[:I] for _ in range(8)])
    idx2 = np.stack([np.random.permutation(T)[:I] for _ in range(8)])
    idx3 = np.stack([np.random.permutation(T)[:I] for _ in range(8)])
    fd = mx_kscale(D)
    keysp = pack_weight(n((D, T)) / fd[:, None], "e4m3")
    return {
        "query": (n((D, Q)) * 0.9 / np.sqrt(D) * fd[:, None]).astype(np.float32),
        "query2": (n((D, Q)) * 0.9 / np.sqrt(D) * fd[:, None]).astype(np.float32),
        "keys_words": keysp[0],
        "keys_scales": keysp[1],
        "lam": (np.random.uniform(1.0, 2.0, (Q, 1))).astype(np.float32),
        "old": (1.0 * n((Q, T))).astype(np.float32),
        "offs": striped8(idx),
        "offs2": striped8(idx2),
        "offs3": striped8(idx3),
    }


def reference(query, query2, keys_words, keys_scales, lam, old, offs, offs2, offs3):
    idx = unstriped8(offs)
    idx2 = unstriped8(offs2)
    idx3 = unstriped8(offs3)
    keysu = unpack_weight(keys_words, keys_scales, "e4m3")
    queryq = mxq(f64(query), 0, "e4m3")
    a = queryq.T @ keysu
    query2q = mxq(f64(query2), 0, "e4m3")
    b = query2q.T @ keysu
    ra = np.sqrt(softplus(pick8(a, idx, 16)) * softplus(pick8(b, idx, 16)) + 0.1)
    w = ra * f64(lam) - np.abs(pick8(a, idx, 16) - pick8(b, idx, 16))
    f1 = np.zeros((Q, T))
    f1[np.arange(Q)[:, None], idx[np.arange(Q) % 128 // 16]] = w
    f2 = f1 + f64(old)
    y = np.maximum(pick8(f2, idx2, 16), pick8(f2, idx3, 16))
    return y

@@ -1,0 +1,143 @@
+from contextlib import ExitStack
+
+import concourse.mybir as mybir
+
+D, T, I, Q = 512, 1024, 512, 128
+FLOPS = 2 * 2 * D * Q * T
+
+F32 = mybir.dt.float32
+BF16 = mybir.dt.bfloat16
+I32 = mybir.dt.int32
+U32 = mybir.dt.uint32
+U16 = mybir.dt.uint16
+U8 = mybir.dt.uint8
+FP8X4 = mybir.dt.float8_e4m3fn_x4
+ALU = mybir.AluOpType
+ACT = mybir.ActivationFunctionType
+
+P = 128
+PACK = 4
+PER_COLUMN = 16
+KEY_HALF = T // 2
+TOKEN_PIECES = ((0, 256), (256, 256), (512, 256), (768, 256))
+HALF = I // 2
+FIRST = 128
+TINY = 2.0 ** -40
+
+
+def listed(offsets, first, last):
+    return offsets[:, first // PER_COLUMN : last // PER_COLUMN]
+
+
+def tile_attend_agreeingtwo_lean_throughtwo_heads_kernel(
+    tc, query, query2, keys_words, keys_scales, lam, old, offs, offs2, offs3, out
+):
+    nc = tc.nc
+    with ExitStack() as ctx:
+        pool = ctx.enter_context(tc.tile_pool(name="pool", bufs=1))
+        psum = ctx.enter_context(tc.psum_pool(name="psum", bufs=1))
+
+        key_scales = pool.tile([P, T], U8, name="key_scales", align_bytes=64)
+        nc.vector.memset(key_scales[:].bitcast(U32), 0)
+
+        raw = [pool.tile([P, PACK, Q], F32, name="raw%d" % n) for n in range(2)]
+        key_words = [pool.tile([P, KEY_HALF], U32, name="key_words%d" % n, tag="key_words%d" % n, align_bytes=64) for n in range(2)]
+        word_rows = keys_words[0].rearrange("p n t -> p (n t)")
+        for n, source in enumerate((query, query2)):
+            nc.sync.dma_start(out=raw[n][:], in_=source.rearrange("(p j) q -> p j q", j=PACK))
+            nc.sync.dma_start(
+                out=key_words[n][:].bitcast(I32),
+                in_=word_rows[:, n * KEY_HALF * PACK : (n + 1) * KEY_HALF * PACK].bitcast(I32),
+            )
+        for quadrant in range(4):
+            nc.scalar.dma_start(
+                out=key_scales[32 * quadrant : 32 * quadrant + 4, :].bitcast(I32),
+                in_=keys_scales[0][4 * quadrant : 4 * quadrant + 4, :].bitcast(I32),
+            )
+        lists = [pool.tile([P, I // PER_COLUMN], U16, name="lists%d" % n) for n in range(3)]
+        nc.sync.dma_start(lists[0][:], offs)
+        lam_col = pool.tile([P, 1], F32, name="lam_col")
+        nc.gpsimd.dma_start(out=lam_col[:], in_=lam)
+        old_totals = pool.tile([P, T], F32, name="old_totals")
+        nc.sync.dma_start(out=old_totals[:], in_=old)
+        nc.sync.dma_start(lists[1][:], offs2)
+        nc.sync.dma_start(lists[2][:], offs3)
+
+        placed = pool.tile([P, T], F32, name="placed")
+        nc.vector.memset(placed[:], 0.0)
+
+        scores = []
+        for n in range(2):
+            grouped = pool.tile([P, Q, PACK], BF16, name="grouped%d" % n, align_bytes=64)
+            nc.vector.tensor_copy(out=grouped[:], in_=raw[n][:].rearrange("p j q -> p q j"))
+            codes = pool.tile([P, Q], U32, name="codes%d" % n, align_bytes=64)
+            scales = pool.tile([P, Q], U8, name="scales%d" % n, align_bytes=64)
+            nc.vector.quantize_mx(
+                out=codes[:].bitcast(FP8X4), scales=scales[:], in_=grouped[:].rearrange("p q j -> p (q j)")
+            )
+            score = pool.tile([P, T], F32, name="score%d" % n)
+            for piece, (first, width) in enumerate(TOKEN_PIECES):
+                bank = psum.tile([P, width], F32, name="bank%d_%d" % (n, first))
+                inside = first % KEY_HALF
+                nc.tensor.matmul_mx(
+                    out=bank[:],
+                    lhsT=codes[:].bitcast(FP8X4),
+                    lhsT_scale=scales[:],
+                    rhs=key_words[first // KEY_HALF][:, inside : inside + width].bitcast(FP8X4),
+                    rhs_scale=key_scales[:, first : first + width],
+                    start=True,
+                    stop=True,
+                )
+                if n == 0 and piece % 2 == 1:
+                    nc.vector.tensor_copy(out=score[:, first : first + width], in_=bank[:])
+                else:
+                    nc.scalar.copy(out=score[:, first : first + width], in_=bank[:])
+            scores.append(score)
+
+        picked = pool.tile([P, 2, I], F32, name="picked")
+        sig = pool.tile([P, 2, I], F32, name="sig", tag="key_words1", align_bytes=64)
+        nc.vector.tensor_copy(picked[:, 0, :], scores[0][:].indirect(lists[0][:]))
+        nc.scalar.activation(sig[:, 0, :], picked[:, 0, :], ACT.Sigmoid, scale=-1.0)
+        for first in (0, HALF):
+            cols = slice(first, first + HALF)
+            nc.vector.tensor_copy(picked[:, 1, cols], scores[1][:].indirect(listed(lists[0], first, first + HALF)))
+            nc.scalar.activation(sig[:, 1, cols], picked[:, 1, cols], ACT.Sigmoid, scale=-1.0)
+
+        logs = pool.tile([P, 2, I], F32, name="logs")
+        soft = pool.tile([P, 2, I], F32, name="soft")
+        product = pool.tile([P, I], F32, name="product")
+        for first in (0, HALF):
+            cols = slice(first, first + HALF)
+            nc.scalar.activation(logs[:, :, cols], sig[:, :, cols], ACT.Ln, bias=TINY)
+        for first in (0, HALF):
+            cols = slice(first, first + HALF)
+            nc.vector.scalar_tensor_tensor(soft[:, :, cols], picked[:, :, cols], -1.0, logs[:, :, cols], ALU.mult, ALU.min)
+            nc.vector.tensor_tensor(product[:, cols], soft[:, 0, cols], soft[:, 1, cols], ALU.mult)
+
+        gap = pool.tile([P, I], F32, name="gap")
+        nc.vector.tensor_tensor(gap[:], picked[:, 0, :], picked[:, 1, :], ALU.subtract)
+        minus_abs = pool.tile([P, I], F32, name="minus_abs")
+        nc.vector.scalar_tensor_tensor(minus_abs[:], gap[:], -1.0, gap[:], ALU.mult, ALU.min)
+
+        root = pool.tile([P, I], F32, name="root")
+        weights = pool.tile([P, FIRST], F32, name="weights")
+        scaled = pool.tile([P, I - FIRST], F32, name="scaled")
+        nc.scalar.activation(root[:, 0:FIRST], product[:, 0:FIRST], ACT.Sqrt, bias=0.1)
+        nc.vector.scalar_tensor_tensor(weights[:], root[:, 0:FIRST], lam_col[:], minus_abs[:, 0:FIRST], ALU.mult, ALU.add)
+        nc.vector.tensor_copy(placed[:].indirect(listed(lists[0], 0, FIRST)), weights[:])
+        nc.scalar.activation(root[:, FIRST:I], product[:, FIRST:I], ACT.Sqrt, bias=0.1)
+        nc.scalar.activation(scaled[:], root[:, FIRST:I], ACT.Copy, scale=lam_col[:])
+        nc.vector.tensor_tensor(placed[:].indirect(listed(lists[0], FIRST, I)), scaled[:], minus_abs[:, FIRST:I], ALU.add)
+
+        totals = pool.tile([P, T], F32, name="totals")
+        nc.vector.tensor_tensor(totals[:], placed[:], old_totals[:], ALU.add)
+
+        at2 = pool.tile([P, I], F32, name="at2")
+        at3 = pool.tile([P, I], F32, name="at3")
+        larger = pool.tile([P, I], F32, name="larger")
+        for first in (0, HALF):
+            cols = slice(first, first + HALF)
+            nc.vector.tensor_copy(at2[:, cols], totals[:].indirect(listed(lists[1], first, first + HALF)))
+            nc.scalar.activation(at3[:, cols], totals[:].indirect(listed(lists[2], first, first + HALF)), ACT.Copy)
+            nc.vector.tensor_tensor(larger[:, cols], at2[:, cols], at3[:, cols], ALU.max)
+            nc.sync.dma_start(out=out[:, cols], in_=larger[:, cols])

@@ -66,6 +66,11 @@ def tile_attend_agreeingtwo_lean_throughtwo_heads_kernel(
         placed = pool.tile([P, T], F32, name="placed")
         nc.vector.memset(placed[:], 0.0)
 
+        warm_in = pool.tile([P, 1], F32, name="warm_in")
+        warm_out = pool.tile([P, 1], F32, name="warm_out")
+        nc.vector.memset(warm_in[:], 0.0)
+        nc.scalar.activation(warm_out[:], warm_in[:], ACT.Sigmoid)
+
         scores = []
         for n in range(2):
             grouped = pool.tile([P, Q, PACK], BF16, name="grouped%d" % n, align_bytes=64)

@@ -38,10 +38,10 @@ def tile_attend_agreeingtwo_lean_throughtwo_heads_kernel(
         psum = ctx.enter_context(tc.psum_pool(name="psum", bufs=1))
 
         key_scales = pool.tile([P, T], U8, name="key_scales", align_bytes=64)
-        nc.vector.memset(key_scales[:].bitcast(U32), 0)
+        nc.gpsimd.memset(key_scales[:].bitcast(U32), 0)
 
         raw = [pool.tile([P, PACK, Q], F32, name="raw%d" % n) for n in range(2)]
-        key_words = [pool.tile([P, KEY_HALF], U32, name="key_words%d" % n, tag="key_words%d" % n, align_bytes=64) for n in range(2)]
+        key_words = [pool.tile([P, KEY_HALF], U32, name="key_words%d" % n, align_bytes=64) for n in range(2)]
         word_rows = keys_words[0].rearrange("p n t -> p (n t)")
         for n, source in enumerate((query, query2)):
             nc.sync.dma_start(out=raw[n][:], in_=source.rearrange("(p j) q -> p j q", j=PACK))
@@ -80,8 +80,8 @@ def tile_attend_agreeingtwo_lean_throughtwo_heads_kernel(
             nc.vector.quantize_mx(
                 out=codes[:].bitcast(FP8X4), scales=scales[:], in_=grouped[:].rearrange("p q j -> p (q j)")
             )
-            score = pool.tile([P, T], F32, name="score%d" % n)
-            for piece, (first, width) in enumerate(TOKEN_PIECES):
+            score = pool.tile([P, T], F32, name="score%d" % n, tag="score%d" % n)
+            for first, width in TOKEN_PIECES:
                 bank = psum.tile([P, width], F32, name="bank%d_%d" % (n, first))
                 inside = first % KEY_HALF
                 nc.tensor.matmul_mx(
@@ -93,22 +93,23 @@ def tile_attend_agreeingtwo_lean_throughtwo_heads_kernel(
                     start=True,
                     stop=True,
                 )
-                if n == 0 and piece % 2 == 1:
-                    nc.vector.tensor_copy(out=score[:, first : first + width], in_=bank[:])
-                else:
+                if n == 0:
                     nc.scalar.copy(out=score[:, first : first + width], in_=bank[:])
+                else:
+                    nc.vector.tensor_copy(out=score[:, first : first + width], in_=bank[:])
             scores.append(score)
 
-        picked = pool.tile([P, 2, I], F32, name="picked")
-        sig = pool.tile([P, 2, I], F32, name="sig", tag="key_words1", align_bytes=64)
-        nc.vector.tensor_copy(picked[:, 0, :], scores[0][:].indirect(lists[0][:]))
-        nc.scalar.activation(sig[:, 0, :], picked[:, 0, :], ACT.Sigmoid, scale=-1.0)
-        for first in (0, HALF):
-            cols = slice(first, first + HALF)
-            nc.vector.tensor_copy(picked[:, 1, cols], scores[1][:].indirect(listed(lists[0], first, first + HALF)))
-            nc.scalar.activation(sig[:, 1, cols], picked[:, 1, cols], ACT.Sigmoid, scale=-1.0)
+        picked_b = pool.tile([P, I], F32, name="picked_b")
+        sig = pool.tile([P, 2, I], F32, name="sig")
+        nc.scalar.activation(sig[:, 0, :], scores[0][:].indirect(lists[0][:]), ACT.Sigmoid, scale=-1.0)
+        nc.vector.tensor_copy(picked_b[:, 0:HALF], scores[1][:].indirect(listed(lists[0], 0, HALF)))
+        nc.scalar.activation(sig[:, 1, HALF:I], scores[1][:].indirect(listed(lists[0], HALF, I)), ACT.Sigmoid, scale=-1.0)
+        nc.scalar.activation(sig[:, 1, 0:HALF], picked_b[:, 0:HALF], ACT.Sigmoid, scale=-1.0)
+        nc.vector.tensor_copy(picked_b[:, HALF:I], scores[1][:].indirect(listed(lists[0], HALF, I)))
+        picked_a = pool.tile([P, I], F32, name="picked_a", tag="score1")
+        nc.vector.tensor_copy(picked_a[:], scores[0][:].indirect(lists[0][:]))
 
-        logs = pool.tile([P, 2, I], F32, name="logs")
+        logs = pool.tile([P, 2, I], F32, name="logs", tag="logs")
         soft = pool.tile([P, 2, I], F32, name="soft")
         product = pool.tile([P, I], F32, name="product")
         for first in (0, HALF):
@@ -116,12 +117,15 @@ def tile_attend_agreeingtwo_lean_throughtwo_heads_kernel(
             nc.scalar.activation(logs[:, :, cols], sig[:, :, cols], ACT.Ln, bias=TINY)
         for first in (0, HALF):
             cols = slice(first, first + HALF)
-            nc.vector.scalar_tensor_tensor(soft[:, :, cols], picked[:, :, cols], -1.0, logs[:, :, cols], ALU.mult, ALU.min)
+            for n, picked in enumerate((picked_a, picked_b)):
+                nc.vector.scalar_tensor_tensor(soft[:, n, cols], picked[:, cols], -1.0, logs[:, n, cols], ALU.mult, ALU.min)
+        for first in (0, HALF):
+            cols = slice(first, first + HALF)
             nc.vector.tensor_tensor(product[:, cols], soft[:, 0, cols], soft[:, 1, cols], ALU.mult)
 
         gap = pool.tile([P, I], F32, name="gap")
-        nc.vector.tensor_tensor(gap[:], picked[:, 0, :], picked[:, 1, :], ALU.subtract)
-        minus_abs = pool.tile([P, I], F32, name="minus_abs")
+        nc.vector.tensor_tensor(gap[:], picked_a[:], picked_b[:], ALU.subtract)
+        minus_abs = pool.tile([P, I], F32, name="minus_abs", tag="logs")
         nc.vector.scalar_tensor_tensor(minus_abs[:], gap[:], -1.0, gap[:], ALU.mult, ALU.min)
 
         root = pool.tile([P, I], F32, name="root")
@@ -140,9 +144,9 @@ def tile_attend_agreeingtwo_lean_throughtwo_heads_kernel(
         at2 = pool.tile([P, I], F32, name="at2")
         at3 = pool.tile([P, I], F32, name="at3")
         larger = pool.tile([P, I], F32, name="larger")
+        nc.vector.tensor_copy(at2[:], totals[:].indirect(lists[1][:]))
         for first in (0, HALF):
             cols = slice(first, first + HALF)
-            nc.vector.tensor_copy(at2[:, cols], totals[:].indirect(listed(lists[1], first, first + HALF)))
             nc.scalar.activation(at3[:, cols], totals[:].indirect(listed(lists[2], first, first + HALF)), ACT.Copy)
             nc.vector.tensor_tensor(larger[:, cols], at2[:, cols], at3[:, cols], ALU.max)
             nc.sync.dma_start(out=out[:, cols], in_=larger[:, cols])

@@ -19,7 +19,7 @@ P = 128
 PACK = 4
 PER_COLUMN = 16
 KEY_HALF = T // 2
-TOKEN_PIECES = ((0, 256), (256, 256), (512, 256), (768, 256))
+TOKEN_PIECES = (((0, 256), (256, 256), (512, 256), (768, 128), (896, 128)), ((0, 256), (256, 256), (512, 256), (768, 256)))
 HALF = I // 2
 FIRST = 128
 TINY = 2.0 ** -40
@@ -56,12 +56,12 @@ def tile_attend_agreeingtwo_lean_throughtwo_heads_kernel(
             )
         lists = [pool.tile([P, I // PER_COLUMN], U16, name="lists%d" % n) for n in range(3)]
         nc.sync.dma_start(lists[0][:], offs)
-        lam_col = pool.tile([P, 1], F32, name="lam_col")
-        nc.gpsimd.dma_start(out=lam_col[:], in_=lam)
         old_totals = pool.tile([P, T], F32, name="old_totals")
         nc.sync.dma_start(out=old_totals[:], in_=old)
         nc.sync.dma_start(lists[1][:], offs2)
         nc.sync.dma_start(lists[2][:], offs3)
+        lam_col = pool.tile([P, 1], F32, name="lam_col")
+        nc.sync.dma_start(out=lam_col[:], in_=lam)
 
         placed = pool.tile([P, T], F32, name="placed")
         nc.vector.memset(placed[:], 0.0)
@@ -81,8 +81,8 @@ def tile_attend_agreeingtwo_lean_throughtwo_heads_kernel(
                 out=codes[:].bitcast(FP8X4), scales=scales[:], in_=grouped[:].rearrange("p q j -> p (q j)")
             )
             score = pool.tile([P, T], F32, name="score%d" % n, tag="score%d" % n)
-            for first, width in TOKEN_PIECES:
-                bank = psum.tile([P, width], F32, name="bank%d_%d" % (n, first))
+            for first, width in TOKEN_PIECES[n]:
+                bank = psum.tile([P, width], F32, name="bank", tag="bank", bufs=8)
                 inside = first % KEY_HALF
                 nc.tensor.matmul_mx(
                     out=bank[:],
@@ -93,7 +93,7 @@ def tile_attend_agreeingtwo_lean_throughtwo_heads_kernel(
                     start=True,
                     stop=True,
                 )
-                if n == 0:
+                if n == 0 and first != 768:
                     nc.scalar.copy(out=score[:, first : first + width], in_=bank[:])
                 else:
                     nc.vector.tensor_copy(out=score[:, first : first + width], in_=bank[:])
@@ -126,7 +126,8 @@ def tile_attend_agreeingtwo_lean_throughtwo_heads_kernel(
         gap = pool.tile([P, I], F32, name="gap")
         nc.vector.tensor_tensor(gap[:], picked_a[:], picked_b[:], ALU.subtract)
         minus_abs = pool.tile([P, I], F32, name="minus_abs", tag="logs")
-        nc.vector.scalar_tensor_tensor(minus_abs[:], gap[:], -1.0, gap[:], ALU.mult, ALU.min)
+        for cols in (slice(0, FIRST), slice(FIRST, I)):
+            nc.vector.scalar_tensor_tensor(minus_abs[:, cols], gap[:, cols], -1.0, gap[:, cols], ALU.mult, ALU.min)
 
         root = pool.tile([P, I], F32, name="root")
         weights = pool.tile([P, FIRST], F32, name="weights")
@@ -144,9 +145,9 @@ def tile_attend_agreeingtwo_lean_throughtwo_heads_kernel(
         at2 = pool.tile([P, I], F32, name="at2")
         at3 = pool.tile([P, I], F32, name="at3")
         larger = pool.tile([P, I], F32, name="larger")
-        nc.vector.tensor_copy(at2[:], totals[:].indirect(lists[1][:]))
         for first in (0, HALF):
             cols = slice(first, first + HALF)
+            nc.vector.tensor_copy(at2[:, cols], totals[:].indirect(listed(lists[1], first, first + HALF)))
             nc.scalar.activation(at3[:, cols], totals[:].indirect(listed(lists[2], first, first + HALF)), ACT.Copy)
             nc.vector.tensor_tensor(larger[:, cols], at2[:, cols], at3[:, cols], ALU.max)
             nc.sync.dma_start(out=out[:, cols], in_=larger[:, cols])

@@ -19,7 +19,7 @@ P = 128
 PACK = 4
 PER_COLUMN = 16
 KEY_HALF = T // 2
-TOKEN_PIECES = (((0, 256), (256, 256), (512, 256), (768, 128), (896, 128)), ((0, 256), (256, 256), (512, 256), (768, 256)))
+PIECE = 256
 HALF = I // 2
 FIRST = 128
 TINY = 2.0 ** -40
@@ -38,21 +38,22 @@ def tile_attend_agreeingtwo_lean_throughtwo_heads_kernel(
         psum = ctx.enter_context(tc.psum_pool(name="psum", bufs=1))
 
         key_scales = pool.tile([P, T], U8, name="key_scales", align_bytes=64)
-        nc.gpsimd.memset(key_scales[:].bitcast(U32), 0)
+        nc.vector.memset(key_scales[:].bitcast(U32), 0)
 
         raw = [pool.tile([P, PACK, Q], F32, name="raw%d" % n) for n in range(2)]
         key_words = [pool.tile([P, KEY_HALF], U32, name="key_words%d" % n, align_bytes=64) for n in range(2)]
         word_rows = keys_words[0].rearrange("p n t -> p (n t)")
         for n, source in enumerate((query, query2)):
             nc.sync.dma_start(out=raw[n][:], in_=source.rearrange("(p j) q -> p j q", j=PACK))
+        for quadrant in range(4):
+            nc.sync.dma_start(
+                out=key_scales[32 * quadrant : 32 * quadrant + 4, :].bitcast(I32),
+                in_=keys_scales[0][4 * quadrant : 4 * quadrant + 4, :].bitcast(I32),
+            )
+        for n in range(2):
             nc.sync.dma_start(
                 out=key_words[n][:].bitcast(I32),
                 in_=word_rows[:, n * KEY_HALF * PACK : (n + 1) * KEY_HALF * PACK].bitcast(I32),
-            )
-        for quadrant in range(4):
-            nc.scalar.dma_start(
-                out=key_scales[32 * quadrant : 32 * quadrant + 4, :].bitcast(I32),
-                in_=keys_scales[0][4 * quadrant : 4 * quadrant + 4, :].bitcast(I32),
             )
         lists = [pool.tile([P, I // PER_COLUMN], U16, name="lists%d" % n) for n in range(3)]
         nc.sync.dma_start(lists[0][:], offs)
@@ -71,7 +72,7 @@ def tile_attend_agreeingtwo_lean_throughtwo_heads_kernel(
         nc.vector.memset(warm_in[:], 0.0)
         nc.scalar.activation(warm_out[:], warm_in[:], ACT.Sigmoid)
 
-        scores = []
+        quantised = []
         for n in range(2):
             grouped = pool.tile([P, Q, PACK], BF16, name="grouped%d" % n, align_bytes=64)
             nc.vector.tensor_copy(out=grouped[:], in_=raw[n][:].rearrange("p j q -> p q j"))
@@ -80,37 +81,45 @@ def tile_attend_agreeingtwo_lean_throughtwo_heads_kernel(
             nc.vector.quantize_mx(
                 out=codes[:].bitcast(FP8X4), scales=scales[:], in_=grouped[:].rearrange("p q j -> p (q j)")
             )
-            score = pool.tile([P, T], F32, name="score%d" % n, tag="score%d" % n)
-            for first, width in TOKEN_PIECES[n]:
-                bank = psum.tile([P, width], F32, name="bank", tag="bank", bufs=8)
-                inside = first % KEY_HALF
-                nc.tensor.matmul_mx(
-                    out=bank[:],
-                    lhsT=codes[:].bitcast(FP8X4),
-                    lhsT_scale=scales[:],
-                    rhs=key_words[first // KEY_HALF][:, inside : inside + width].bitcast(FP8X4),
-                    rhs_scale=key_scales[:, first : first + width],
-                    start=True,
-                    stop=True,
-                )
-                if n == 0 and first != 768:
-                    nc.scalar.copy(out=score[:, first : first + width], in_=bank[:])
-                else:
-                    nc.vector.tensor_copy(out=score[:, first : first + width], in_=bank[:])
-            scores.append(score)
+            quantised.append((codes, scales))
+
+        scores = [pool.tile([P, T], F32, name="score%d" % n, tag="score%d" % n) for n in range(2)]
+        for half in range(2):
+            for n, (codes, scales) in enumerate(quantised):
+                for inside in range(0, KEY_HALF, PIECE):
+                    tokens = slice(half * KEY_HALF + inside, half * KEY_HALF + inside + PIECE)
+                    bank = psum.tile([P, PIECE], F32, name="bank", tag="bank", bufs=8)
+                    nc.tensor.matmul_mx(
+                        out=bank[:],
+                        lhsT=codes[:].bitcast(FP8X4),
+                        lhsT_scale=scales[:],
+                        rhs=key_words[half][:, inside : inside + PIECE].bitcast(FP8X4),
+                        rhs_scale=key_scales[:, tokens],
+                        start=True,
+                        stop=True,
+                    )
+                    if n == 0:
+                        nc.scalar.copy(out=scores[n][:, tokens], in_=bank[:])
+                    else:
+                        nc.vector.tensor_copy(out=scores[n][:, tokens], in_=bank[:])
 
         picked_b = pool.tile([P, I], F32, name="picked_b")
         sig = pool.tile([P, 2, I], F32, name="sig")
         nc.scalar.activation(sig[:, 0, :], scores[0][:].indirect(lists[0][:]), ACT.Sigmoid, scale=-1.0)
-        nc.vector.tensor_copy(picked_b[:, 0:HALF], scores[1][:].indirect(listed(lists[0], 0, HALF)))
-        nc.scalar.activation(sig[:, 1, HALF:I], scores[1][:].indirect(listed(lists[0], HALF, I)), ACT.Sigmoid, scale=-1.0)
-        nc.scalar.activation(sig[:, 1, 0:HALF], picked_b[:, 0:HALF], ACT.Sigmoid, scale=-1.0)
-        nc.vector.tensor_copy(picked_b[:, HALF:I], scores[1][:].indirect(listed(lists[0], HALF, I)))
+        for first in (0, HALF):
+            cols = slice(first, first + HALF)
+            nc.vector.tensor_copy(picked_b[:, cols], scores[1][:].indirect(listed(lists[0], first, first + HALF)))
+            nc.scalar.activation(sig[:, 1, cols], picked_b[:, cols], ACT.Sigmoid, scale=-1.0)
         picked_a = pool.tile([P, I], F32, name="picked_a", tag="score1")
         nc.vector.tensor_copy(picked_a[:], scores[0][:].indirect(lists[0][:]))
 
-        logs = pool.tile([P, 2, I], F32, name="logs", tag="logs")
-        soft = pool.tile([P, 2, I], F32, name="soft")
+        gap = pool.tile([P, I], F32, name="gap", tag="gap")
+        nc.vector.tensor_tensor(gap[:], picked_a[:], picked_b[:], ALU.subtract)
+        minus_abs = pool.tile([P, I], F32, name="minus_abs")
+        nc.vector.scalar_tensor_tensor(minus_abs[:], gap[:], -1.0, gap[:], ALU.mult, ALU.min)
+
+        logs = pool.tile([P, 2, I], F32, name="logs")
+        soft = pool.tile([P, 2, I], F32, name="soft", tag="gap")
         product = pool.tile([P, I], F32, name="product")
         for first in (0, HALF):
             cols = slice(first, first + HALF)
@@ -122,12 +131,6 @@ def tile_attend_agreeingtwo_lean_throughtwo_heads_kernel(
         for first in (0, HALF):
             cols = slice(first, first + HALF)
             nc.vector.tensor_tensor(product[:, cols], soft[:, 0, cols], soft[:, 1, cols], ALU.mult)
-
-        gap = pool.tile([P, I], F32, name="gap")
-        nc.vector.tensor_tensor(gap[:], picked_a[:], picked_b[:], ALU.subtract)
-        minus_abs = pool.tile([P, I], F32, name="minus_abs", tag="logs")
-        for cols in (slice(0, FIRST), slice(FIRST, I)):
-            nc.vector.scalar_tensor_tensor(minus_abs[:, cols], gap[:, cols], -1.0, gap[:, cols], ALU.mult, ALU.min)
 
         root = pool.tile([P, I], F32, name="root")
         weights = pool.tile([P, FIRST], F32, name="weights")

from contextlib import ExitStack

import concourse.mybir as mybir

D, T, I, Q = 512, 1024, 512, 128
FLOPS = 2 * 2 * D * Q * T

F32 = mybir.dt.float32
BF16 = mybir.dt.bfloat16
I32 = mybir.dt.int32
U32 = mybir.dt.uint32
U16 = mybir.dt.uint16
U8 = mybir.dt.uint8
FP8X4 = mybir.dt.float8_e4m3fn_x4
ALU = mybir.AluOpType
ACT = mybir.ActivationFunctionType

P = 128
PACK = 4
PER_COLUMN = 16
KEY_HALF = T // 2
PIECE = 256
HALF = I // 2
FIRST = 128
TINY = 2.0 ** -40


def listed(offsets, first, last):
    return offsets[:, first // PER_COLUMN : last // PER_COLUMN]


def tile_attend_agreeingtwo_lean_throughtwo_heads_kernel(
    tc, query, query2, keys_words, keys_scales, lam, old, offs, offs2, offs3, out
):
    nc = tc.nc
    with ExitStack() as ctx:
        pool = ctx.enter_context(tc.tile_pool(name="pool", bufs=1))
        psum = ctx.enter_context(tc.psum_pool(name="psum", bufs=1))

        key_scales = pool.tile([P, T], U8, name="key_scales", align_bytes=64)
        nc.vector.memset(key_scales[:].bitcast(U32), 0)

        raw = [pool.tile([P, PACK, Q], F32, name="raw%d" % n) for n in range(2)]
        key_words = [pool.tile([P, KEY_HALF], U32, name="key_words%d" % n, align_bytes=64) for n in range(2)]
        word_rows = keys_words[0].rearrange("p n t -> p (n t)")
        for n, source in enumerate((query, query2)):
            nc.sync.dma_start(out=raw[n][:], in_=source.rearrange("(p j) q -> p j q", j=PACK))
        for quadrant in range(4):
            nc.sync.dma_start(
                out=key_scales[32 * quadrant : 32 * quadrant + 4, :].bitcast(I32),
                in_=keys_scales[0][4 * quadrant : 4 * quadrant + 4, :].bitcast(I32),
            )
        for n in range(2):
            nc.sync.dma_start(
                out=key_words[n][:].bitcast(I32),
                in_=word_rows[:, n * KEY_HALF * PACK : (n + 1) * KEY_HALF * PACK].bitcast(I32),
            )
        lists = [pool.tile([P, I // PER_COLUMN], U16, name="lists%d" % n) for n in range(3)]
        nc.sync.dma_start(lists[0][:], offs)
        old_totals = pool.tile([P, T], F32, name="old_totals")
        nc.sync.dma_start(out=old_totals[:], in_=old)
        nc.sync.dma_start(lists[1][:], offs2)
        nc.sync.dma_start(lists[2][:], offs3)
        lam_col = pool.tile([P, 1], F32, name="lam_col")
        nc.sync.dma_start(out=lam_col[:], in_=lam)

        placed = pool.tile([P, T], F32, name="placed")
        nc.vector.memset(placed[:], 0.0)

        warm_in = pool.tile([P, 1], F32, name="warm_in")
        warm_out = pool.tile([P, 1], F32, name="warm_out")
        nc.vector.memset(warm_in[:], 0.0)
        nc.scalar.activation(warm_out[:], warm_in[:], ACT.Sigmoid)

        quantised = []
        for n in range(2):
            grouped = pool.tile([P, Q, PACK], BF16, name="grouped%d" % n, align_bytes=64)
            nc.vector.tensor_copy(out=grouped[:], in_=raw[n][:].rearrange("p j q -> p q j"))
            codes = pool.tile([P, Q], U32, name="codes%d" % n, align_bytes=64)
            scales = pool.tile([P, Q], U8, name="scales%d" % n, align_bytes=64)
            nc.vector.quantize_mx(
                out=codes[:].bitcast(FP8X4), scales=scales[:], in_=grouped[:].rearrange("p q j -> p (q j)")
            )
            quantised.append((codes, scales))

        scores = [pool.tile([P, T], F32, name="score%d" % n, tag="score%d" % n) for n in range(2)]
        for half in range(2):
            for n, (codes, scales) in enumerate(quantised):
                for inside in range(0, KEY_HALF, PIECE):
                    tokens = slice(half * KEY_HALF + inside, half * KEY_HALF + inside + PIECE)
                    bank = psum.tile([P, PIECE], F32, name="bank", tag="bank", bufs=8)
                    nc.tensor.matmul_mx(
                        out=bank[:],
                        lhsT=codes[:].bitcast(FP8X4),
                        lhsT_scale=scales[:],
                        rhs=key_words[half][:, inside : inside + PIECE].bitcast(FP8X4),
                        rhs_scale=key_scales[:, tokens],
                        start=True,
                        stop=True,
                    )
                    if n == 0:
                        nc.scalar.copy(out=scores[n][:, tokens], in_=bank[:])
                    else:
                        nc.vector.tensor_copy(out=scores[n][:, tokens], in_=bank[:])

        picked_b = pool.tile([P, I], F32, name="picked_b")
        sig = pool.tile([P, 2, I], F32, name="sig")
        nc.scalar.activation(sig[:, 0, :], scores[0][:].indirect(lists[0][:]), ACT.Sigmoid, scale=-1.0)
        for first in (0, HALF):
            cols = slice(first, first + HALF)
            nc.vector.tensor_copy(picked_b[:, cols], scores[1][:].indirect(listed(lists[0], first, first + HALF)))
            nc.scalar.activation(sig[:, 1, cols], picked_b[:, cols], ACT.Sigmoid, scale=-1.0)
        picked_a = pool.tile([P, I], F32, name="picked_a", tag="score1")
        nc.vector.tensor_copy(picked_a[:], scores[0][:].indirect(lists[0][:]))

        gap = pool.tile([P, I], F32, name="gap", tag="gap")
        nc.vector.tensor_tensor(gap[:], picked_a[:], picked_b[:], ALU.subtract)
        minus_abs = pool.tile([P, I], F32, name="minus_abs")
        nc.vector.scalar_tensor_tensor(minus_abs[:], gap[:], -1.0, gap[:], ALU.mult, ALU.min)

        logs = pool.tile([P, 2, I], F32, name="logs")
        soft = pool.tile([P, 2, I], F32, name="soft", tag="gap")
        product = pool.tile([P, I], F32, name="product")
        for first in (0, HALF):
            cols = slice(first, first + HALF)
            nc.scalar.activation(logs[:, :, cols], sig[:, :, cols], ACT.Ln, bias=TINY)
        for first in (0, HALF):
            cols = slice(first, first + HALF)
            for n, picked in enumerate((picked_a, picked_b)):
                nc.vector.scalar_tensor_tensor(soft[:, n, cols], picked[:, cols], -1.0, logs[:, n, cols], ALU.mult, ALU.min)
        for first in (0, HALF):
            cols = slice(first, first + HALF)
            nc.vector.tensor_tensor(product[:, cols], soft[:, 0, cols], soft[:, 1, cols], ALU.mult)

        root = pool.tile([P, I], F32, name="root")
        weights = pool.tile([P, FIRST], F32, name="weights")
        scaled = pool.tile([P, I - FIRST], F32, name="scaled")
        nc.scalar.activation(root[:, 0:FIRST], product[:, 0:FIRST], ACT.Sqrt, bias=0.1)
        nc.vector.scalar_tensor_tensor(weights[:], root[:, 0:FIRST], lam_col[:], minus_abs[:, 0:FIRST], ALU.mult, ALU.add)
        nc.vector.tensor_copy(placed[:].indirect(listed(lists[0], 0, FIRST)), weights[:])
        nc.scalar.activation(root[:, FIRST:I], product[:, FIRST:I], ACT.Sqrt, bias=0.1)
        nc.scalar.activation(scaled[:], root[:, FIRST:I], ACT.Copy, scale=lam_col[:])
        nc.vector.tensor_tensor(placed[:].indirect(listed(lists[0], FIRST, I)), scaled[:], minus_abs[:, FIRST:I], ALU.add)

        totals = pool.tile([P, T], F32, name="totals")
        nc.vector.tensor_tensor(totals[:], placed[:], old_totals[:], ALU.add)

        at2 = pool.tile([P, I], F32, name="at2")
        at3 = pool.tile([P, I], F32, name="at3")
        larger = pool.tile([P, I], F32, name="larger")
        for first in (0, HALF):
            cols = slice(first, first + HALF)
            nc.vector.tensor_copy(at2[:, cols], totals[:].indirect(listed(lists[1], first, first + HALF)))
            nc.scalar.activation(at3[:, cols], totals[:].indirect(listed(lists[2], first, first + HALF)), ACT.Copy)
            nc.vector.tensor_tensor(larger[:, cols], at2[:, cols], at3[:, cols], ALU.max)
            nc.sync.dma_start(out=out[:, cols], in_=larger[:, cols])
